import numpy as np
import ml_dtypes


def mxq(x, axis, fmt="e4m3"):
    dtype, down = {"e4m3": (ml_dtypes.float8_e4m3fn, 7), "e5m2": (ml_dtypes.float8_e5m2, 14)}[fmt]
    v = np.moveaxis(np.asarray(x, np.float32).astype(ml_dtypes.bfloat16).astype(np.float64), axis, -1)
    blocks = v.reshape(v.shape[:-1] + (-1, 32))
    amax = np.abs(blocks).max(-1, keepdims=True)
    byte = np.maximum(np.where(amax > 0, np.frexp(amax)[1] - 1 + 127, 0) - down, 1)
    scale = np.exp2(byte - 127.0)
    codes = (blocks / scale).astype(np.float32).astype(dtype).astype(np.float64)
    return np.moveaxis((codes * scale).reshape(v.shape), -1, axis)


WIDE = False


def mx_kscale(k):
    if not WIDE:
        return np.ones(k)
    levels = np.array([10, -10, 5, -5, 0])
    if k % 512:
        return np.exp2(np.random.permutation(np.resize(levels, k // 32))).repeat(32)
    a = np.empty((k // 512, 16))
    for p in range(k // 512):
        a[p, :8] = np.random.permutation(np.resize(levels, 8))
        for g in range(8):
            far = levels[np.abs(levels - a[p, g]) >= 10]
            a[p, g + 8] = far[np.random.randint(len(far))]
    return np.exp2(a.ravel()).repeat(32)


def f64(x):
    return np.asarray(x).astype(np.float64)


def striped8(idx):
    return np.asarray(idx).reshape(8, -1, 16).transpose(0, 2, 1).reshape(128, -1).astype(np.uint16)


def unstriped8(offs):
    return offs.reshape(8, 16, -1).transpose(0, 2, 1).reshape(8, -1).astype(np.int64)


def pick8(x, idx, run):
    r = np.arange(len(x))
    return x[r[:, None], idx[r % (8 * run) // run]]


E2M1 = np.array([0.0, 0.5, 1.0, 1.5, 2.0, 3.0, 4.0, 6.0, -0.0, -0.5, -1.0, -1.5, -2.0, -3.0, -4.0, -6.0])


def pack_weight(w, fmt):
    k, n = w.shape
    w = f64(np.asarray(w, np.float32).astype(ml_dtypes.bfloat16)).reshape(k // 32, 32, n)
    amax = np.abs(w).max(1)
    if fmt == "e4m3":
        byte = np.frexp(amax)[1] - 1 + 127 - 7
    else:
        mant, ex = np.frexp(amax / 6.0)
        byte = np.where(mant > 0.5, ex, ex - 1) + 127
    byte = np.clip(np.where(amax > 0, byte, 1), 1, 254)
    scaled = (w * np.exp2(127.0 - byte)[:, None, :]).reshape(k, n).astype(np.float32)
    by_word = np.ascontiguousarray(scaled.reshape(k // 512, 128, 4, n).transpose(0, 1, 3, 2))
    if fmt == "e4m3":
        words = by_word.astype(ml_dtypes.float8_e4m3fn).view(np.uint8)
    else:
        c = by_word.astype(ml_dtypes.float4_e2m1fn).view(np.uint8) & 0xF
        words = (c[..., 0::2] | (c[..., 1::2] << 4)).reshape(k // 512, 128, 2 * n)
    return np.ascontiguousarray(words), np.ascontiguousarray(byte.astype(np.uint8).reshape(k // 512, 16, n))


def unpack_weight(words, scales, fmt):
    g, _, n = scales.shape
    words = np.ascontiguousarray(words).reshape(g, 128, n, -1)
    if fmt == "e4m3":
        vals = words.view(ml_dtypes.float8_e4m3fn).astype(np.float64)
    else:
        nib = np.empty((g, 128, n, 4), np.uint8)
        nib[..., 0::2] = words & 0xF
        nib[..., 1::2] = words >> 4
        vals = E2M1[nib]
    vals = vals * np.repeat(np.exp2(scales.astype(np.float64) - 127.0), 8, axis=1)[..., None]
    return vals.transpose(0, 1, 3, 2).reshape(g * 512, n)


def bf(x):
    return np.asarray(x, np.float32).astype(ml_dtypes.bfloat16)


def planes(Y):
    r, m = Y.shape
    b = f64(bf(Y)).reshape(r // 32, 32, m)
    amax = np.abs(b).max(1)
    byte = np.clip(np.where(amax > 0, np.frexp(amax)[1] - 1 + 127 - 7, 1), 1, 254)
    codes = (b * np.exp2(127.0 - byte)[:, None, :]).reshape(r, m).astype(np.float32).astype(ml_dtypes.float8_e4m3fn).view(np.uint8)
    words = codes.reshape(r // 512, 128, 4, m).transpose(0, 1, 3, 2)
    return np.ascontiguousarray(words), np.ascontiguousarray(byte.astype(np.uint8).reshape(r // 512, 16, m))


K, L, T, J, N = 1024, 512, 1024, 512, 512


def setup_inputs():
    n = np.random.standard_normal
    idx = np.stack([np.random.permutation(T)[:J] for _ in range(8)])
    idx2 = np.stack([np.random.permutation(T)[:J] for _ in range(8)])
    fk = mx_kscale(K)
    fl = mx_kscale(L)
    xap = pack_weight(n((K, J)) / fk[:, None], "e2m1")
    xbp = pack_weight(n((L, J)) / fl[:, None], "e4m3")
    wbp = pack_weight(n((L, N)) * 1 / np.sqrt(L) * fl[:, None], "e2m1")
    return {
        "xa_words": xap[0],
        "xa_scales": xap[1],
        "wa": (n((K, N)) * 1 / np.sqrt(K) * fk[:, None]).astype(np.float32),
        "xb_words": xbp[0],
        "xb_scales": xbp[1],
        "wb_words": wbp[0],
        "wb_scales": wbp[1],
        "res": (1.0 * n((N, T))).astype(np.float32),
        "offs": striped8(idx),
        "offs2": striped8(idx2),
    }


def reference(xa_words, xa_scales, wa, xb_words, xb_scales, wb_words, wb_scales, res, offs, offs2):
    idx = unstriped8(offs)
    idx2 = unstriped8(offs2)
    xau = unpack_weight(xa_words, xa_scales, "e2m1")
    xbu = unpack_weight(xb_words, xb_scales, "e4m3")
    wbu = unpack_weight(wb_words, wb_scales, "e2m1")
    waq = mxq(f64(wa), 0, "e4m3")
    p = waq.T @ xau
    q = wbu.T @ xbu
    pg = np.zeros((N, T))
    pg[np.arange(N)[:, None], idx[np.arange(N) % 512 // 64]] = p
    qg = np.zeros((N, T))
    qg[np.arange(N)[:, None], idx2[np.arange(N) % 512 // 64]] = q
    y = np.maximum(pg, qg) + 0.3 * f64(res)
    words, scales = planes(y)
    return y, words, scales

@@ -1,0 +1,230 @@
+from contextlib import ExitStack
+
+import concourse.mybir as mybir
+
+K, L, T, J, N = 1024, 512, 1024, 512, 512
+FLOPS = 2 * (K + L) * N * J
+
+F32 = mybir.dt.float32
+BF16 = mybir.dt.bfloat16
+I32 = mybir.dt.int32
+U32 = mybir.dt.uint32
+U16 = mybir.dt.uint16
+U8 = mybir.dt.uint8
+FP8X4 = mybir.dt.float8_e4m3fn_x4
+FP4X4 = mybir.dt.float4_e2m1fn_x4
+ALU = mybir.AluOpType
+COPY = mybir.ActivationFunctionType.Copy
+
+P = 128
+PACK = 4
+K_PASS = P * PACK
+PASSES = K // K_PASS
+QUADS = 4
+HALF = T // 2
+LEAD = 128
+
+
+def tile_moe_heads_of_two_experts_pl_kernel(
+    tc, xa_words, xa_scales, wa, xb_words, xb_scales, wb_words, wb_scales, res, offs, offs2, out_0, out_1, out_2
+):
+    nc = tc.nc
+    with ExitStack() as ctx:
+        lists = ctx.enter_context(tc.tile_pool(name="lists", bufs=1))
+        sb = ctx.enter_context(tc.tile_pool(name="sb", bufs=1))
+        psum = ctx.enter_context(tc.psum_pool(name="psum", bufs=1))
+
+        def sbuf(name, shape, dtype, tag=None):
+            return sb.tile(shape, dtype, name=name, tag=tag or name, align_bytes=64)
+
+        list_p = lists.tile([P, J // 16], U16, name="list_p")
+        list_q = lists.tile([P, J // 16], U16, name="list_q")
+
+        wb_raw = sbuf("wb_raw", [P, 2 * N], U8, tag="wb_wa_res")
+        wb_scale_raw = sbuf("wb_scale_raw", [P, N], U8, tag="scale_wa_q")
+        xb_codes = sbuf("xb_codes", [P, J], U32, tag="xb_win0")
+        xb_scale = sbuf("xb_scale", [P, J], U8, tag="xb_win1")
+
+        nc.vector.memset(wb_scale_raw[:].bitcast(I32), 0)
+        nc.vector.memset(xb_scale[:].bitcast(I32), 0)
+
+        nc.sync.dma_start(out=wb_raw[:].bitcast(I32), in_=wb_words[0].bitcast(I32))
+        nc.scalar.dma_start(
+            out=xb_codes[:].bitcast(I32), in_=xb_words[0].rearrange("p n t -> p (n t)").bitcast(I32)
+        )
+        for q in range(QUADS):
+            (nc.sync if q % 2 == 0 else nc.scalar).dma_start(
+                out=wb_scale_raw[32 * q : 32 * q + 4, :].bitcast(I32),
+                in_=wb_scales[0, 4 * q : 4 * q + 4, :].bitcast(I32),
+            )
+        for q in range(QUADS):
+            nc.sync.dma_start(
+                out=xb_scale[32 * q : 32 * q + 4, :].bitcast(I32),
+                in_=xb_scales[0, 4 * q : 4 * q + 4, :].bitcast(I32),
+            )
+        nc.sync.dma_start(list_q[:], offs2)
+
+        nc.sync.dma_start(list_p[:], offs)
+        res_rows = res.rearrange("(p t) c -> p t c", t=PACK)
+        out_rows = out_0.rearrange("(p t) c -> t p c", t=PACK)
+
+        q_win = []
+        for t in range(PACK):
+            win = sbuf(f"q_win{t}", [P, T], F32)
+            nc.vector.memset(win[:], 0.0)
+            q_win.append(win)
+
+        wb_codes = sbuf("wb_codes", [P, 2 * N], U8, tag="wb_xa_codes")
+        wb_scale = sbuf("wb_scale", [P, N], U8, tag="wb_xa_scale")
+        nc.vector.tensor_copy(
+            out=wb_codes[:].bitcast(U16).rearrange("p (t m) -> p t m", t=PACK),
+            in_=wb_raw[:].bitcast(U16).rearrange("p (m t) -> p t m", t=PACK),
+        )
+        nc.vector.tensor_copy(
+            out=wb_scale[:].rearrange("p (t m) -> p t m", t=PACK),
+            in_=wb_scale_raw[:].rearrange("p (m t) -> p t m", t=PACK),
+        )
+
+        wa_raw = []
+        for z, tag in enumerate(("wb_wa_res", "scale_wa_q")):
+            raw = sbuf(f"wa_raw{z}", [P, PACK, N], F32, tag=tag)
+            nc.sync.dma_start(
+                out=raw[:], in_=wa[z * K_PASS : (z + 1) * K_PASS, :].rearrange("(p j) n -> p j n", j=PACK)
+            )
+            wa_raw.append(raw)
+
+        q_bank = []
+        for t in range(PACK):
+            bank = psum.tile([P, J], F32, name=f"q_bank{t}")
+            nc.tensor.matmul_mx(
+                out=bank[:],
+                lhsT=wb_codes[:, 2 * P * t : 2 * P * (t + 1)].bitcast(FP4X4),
+                lhsT_scale=wb_scale[:, P * t : P * (t + 1)],
+                rhs=xb_codes[:].bitcast(FP8X4),
+                rhs_scale=xb_scale[:],
+                start=True,
+                stop=True,
+            )
+            q_bank.append(bank)
+
+        def scatter_q(t, tag):
+            slots = sbuf(f"q_slots{t}", [P, J], F32, tag=tag)
+            nc.scalar.copy(out=slots[:], in_=q_bank[t][:])
+            nc.vector.tensor_copy(out=q_win[t][:].indirect(list_q[:]), in_=slots[:])
+
+        for t in range(PACK - 1):
+            scatter_q(t, None)
+
+        xa_codes = sbuf("xa_codes", [P, PASSES, 2 * J], U8, tag="wb_xa_codes")
+        xa_scale = sbuf("xa_scale", [P, PASSES, J], U8, tag="wb_xa_scale")
+        nc.gpsimd.memset(xa_scale[:].bitcast(I32), 0)
+        nc.sync.dma_start(out=xa_codes[:].bitcast(I32), in_=xa_words.bitcast(I32).rearrange("z p w -> p z w"))
+        for q in range(QUADS):
+            nc.sync.dma_start(
+                out=xa_scale[32 * q : 32 * q + 4, :, :].bitcast(I32),
+                in_=xa_scales[:, 4 * q : 4 * q + 4, :].bitcast(I32).rearrange("z r w -> r z w"),
+            )
+
+        p_win = []
+        for b in range(2):
+            win = sbuf(f"p_win{b}", [P, T], F32, tag=f"xb_win{b}")
+            nc.gpsimd.memset(win[:], 0.0)
+            p_win.append(win)
+
+        wa_codes, wa_scale = [], []
+        for z in range(PASSES):
+            grouped = sbuf(f"wa_grouped{z}", [P, PACK * N], BF16)
+            nc.scalar.copy(
+                out=grouped[:].rearrange("p (t m j) -> p m t j", t=PACK, j=PACK),
+                in_=wa_raw[z][:].rearrange("p j (m t) -> p m t j", t=PACK),
+            )
+            codes = sbuf(f"wa_codes{z}", [P, N], U32)
+            scale = sbuf(f"wa_scale{z}", [P, N], U8)
+            nc.vector.quantize_mx(out=codes[:].bitcast(FP8X4), scales=scale[:], in_=grouped[:])
+            wa_codes.append(codes)
+            wa_scale.append(scale)
+
+        res_raw = sbuf("res_raw", [P, PACK, T], F32, tag="wb_wa_res")
+        nc.sync.dma_start(out=res_raw[:], in_=res_rows)
+
+        scatter_q(PACK - 1, "scale_wa_q")
+
+        p_slots = []
+        for t in range(PACK):
+            bank = psum.tile([P, J], F32, name=f"p_bank{t}")
+            for z in range(PASSES):
+                nc.tensor.matmul_mx(
+                    out=bank[:],
+                    lhsT=wa_codes[z][:, P * t : P * (t + 1)].bitcast(FP8X4),
+                    lhsT_scale=wa_scale[z][:, P * t : P * (t + 1)],
+                    rhs=xa_codes[:, z, :].bitcast(FP4X4),
+                    rhs_scale=xa_scale[:, z, :],
+                    start=(z == 0),
+                    stop=(z == PASSES - 1),
+                )
+            slots = sbuf(f"p_slots{t}", [P, J], F32)
+            nc.scalar.copy(out=slots[:], in_=bank[:])
+            p_slots.append(slots)
+
+        res_scaled = []
+        for t in range(PACK):
+            scaled = sbuf(f"res_scaled{t}", [P, T], F32)
+            nc.scalar.activation(out=scaled[:], in_=res_raw[:, t, :], func=COPY, scale=0.3)
+            res_scaled.append(scaled)
+
+        y_pair = [sbuf(f"y_pair{u}", [P, 2, T], F32) for u in range(2)]
+        y_bf = [sbuf(f"y_bf{h}", [P, HALF, PACK], BF16) for h in range(2)]
+        halves = [slice(h * HALF, (h + 1) * HALF) for h in range(2)]
+        larger = [sbuf(f"larger{t}", [P, T], F32) for t in range(PACK)]
+
+        def scatter_p(t, lo, hi):
+            nc.vector.tensor_copy(
+                out=p_win[t % 2][:].indirect(list_p[:, lo // 16 : hi // 16]), in_=p_slots[t][:, lo:hi]
+            )
+
+        def combine(t):
+            y = y_pair[t // 2][:, t % 2, :]
+            nc.vector.tensor_tensor(out=larger[t][:], in0=p_win[t % 2][:], in1=q_win[t][:], op=ALU.max)
+            nc.gpsimd.tensor_tensor(out=y, in0=larger[t][:], in1=res_scaled[t][:], op=ALU.add)
+            nc.sync.dma_start(out=out_rows[t], in_=y)
+
+        scatter_p(0, 0, J)
+        for t in range(1, PACK):
+            scatter_p(t, 0, LEAD)
+            combine(t - 1)
+            scatter_p(t, LEAD, J)
+            if t == 2:
+                for h in range(2):
+                    nc.scalar.copy(
+                        out=y_bf[h][:, :, 0:2], in_=y_pair[0][:, :, halves[h]].rearrange("p e c -> p c e")
+                    )
+
+        last = PACK - 1
+        y = y_pair[1][:, 1, :]
+        for cols in halves:
+            nc.vector.tensor_tensor(
+                out=larger[last][:, cols], in0=p_win[1][:, cols], in1=q_win[last][:, cols], op=ALU.max
+            )
+        for cols in halves:
+            nc.vector.tensor_tensor(
+                out=y[:, cols], in0=larger[last][:, cols], in1=res_scaled[last][:, cols], op=ALU.add
+            )
+            nc.sync.dma_start(out=out_rows[last][:, cols], in_=y[:, cols])
+
+        nc.scalar.copy(out=y_bf[0][:, :, 2:4], in_=y_pair[1][:, :, halves[0]].rearrange("p e c -> p c e"))
+        nc.vector.tensor_copy(out=y_bf[1][:, :, 2:4], in_=y_pair[1][:, :, halves[1]].rearrange("p e c -> p c e"))
+
+        y_scale = sbuf("y_scale", [P, T], U8)
+        words_out = out_1[0].rearrange("p c t -> p (c t)").bitcast(I32)
+        for h in (1, 0):
+            codes = sbuf(f"y_codes{h}", [P, HALF], U32)
+            nc.vector.quantize_mx(
+                out=codes[:].bitcast(FP8X4),
+                scales=y_scale[:, halves[h]],
+                in_=y_bf[h][:].rearrange("p c t -> p (c t)"),
+            )
+            nc.sync.dma_start(out=words_out[:, halves[h]], in_=codes[:].bitcast(I32))
+        for q in range(QUADS):
+            nc.scalar.dma_start(
+                out=out_2[0, 4 * q : 4 * q + 4, :].bitcast(I32), in_=y_scale[32 * q : 32 * q + 4, :].bitcast(I32)
+            )

@@ -21,7 +21,8 @@ PACK = 4
 K_PASS = P * PACK
 PASSES = K // K_PASS
 QUADS = 4
-HALF = T // 2
+CHUNKS = 4
+CHUNK = T // CHUNKS
 LEAD = 128
 
 
@@ -40,50 +41,30 @@ def tile_moe_heads_of_two_experts_pl_kernel(
         list_p = lists.tile([P, J // 16], U16, name="list_p")
         list_q = lists.tile([P, J // 16], U16, name="list_q")
 
-        wb_raw = sbuf("wb_raw", [P, 2 * N], U8, tag="wb_wa_res")
-        wb_scale_raw = sbuf("wb_scale_raw", [P, N], U8, tag="scale_wa_q")
-        xb_codes = sbuf("xb_codes", [P, J], U32, tag="xb_win0")
-        xb_scale = sbuf("xb_scale", [P, J], U8, tag="xb_win1")
+        wb_raw = sbuf("wb_raw", [P, 2 * N], U8, tag="then_q_win1")
+        wb_scale_raw = sbuf("wb_scale_raw", [P, N], U8, tag="then_q_win2")
+        xb_codes = sbuf("xb_codes", [P, J], U32, tag="then_q_win3")
+        xb_scale = sbuf("xb_scale", [P, J], U8, tag="then_p_win0")
 
-        nc.vector.memset(wb_scale_raw[:].bitcast(I32), 0)
-        nc.vector.memset(xb_scale[:].bitcast(I32), 0)
+        nc.gpsimd.memset(wb_scale_raw[:].bitcast(I32), 0)
 
+        def load_scale_rows(plane, rows, q):
+            nc.sync.dma_start(
+                out=plane[32 * q : 32 * q + 4, :].bitcast(I32), in_=rows[4 * q : 4 * q + 4, :].bitcast(I32)
+            )
+
+        nc.sync.dma_start(list_q[:], offs2)
+        nc.sync.dma_start(list_p[:], offs)
+        for q in range(2):
+            load_scale_rows(xb_scale, xb_scales[0], q)
         nc.sync.dma_start(out=wb_raw[:].bitcast(I32), in_=wb_words[0].bitcast(I32))
-        nc.scalar.dma_start(
+        nc.sync.dma_start(
             out=xb_codes[:].bitcast(I32), in_=xb_words[0].rearrange("p n t -> p (n t)").bitcast(I32)
         )
+        for q in range(2, QUADS):
+            load_scale_rows(xb_scale, xb_scales[0], q)
         for q in range(QUADS):
-            (nc.sync if q % 2 == 0 else nc.scalar).dma_start(
-                out=wb_scale_raw[32 * q : 32 * q + 4, :].bitcast(I32),
-                in_=wb_scales[0, 4 * q : 4 * q + 4, :].bitcast(I32),
-            )
-        for q in range(QUADS):
-            nc.sync.dma_start(
-                out=xb_scale[32 * q : 32 * q + 4, :].bitcast(I32),
-                in_=xb_scales[0, 4 * q : 4 * q + 4, :].bitcast(I32),
-            )
-        nc.sync.dma_start(list_q[:], offs2)
-
-        nc.sync.dma_start(list_p[:], offs)
-        res_rows = res.rearrange("(p t) c -> p t c", t=PACK)
-        out_rows = out_0.rearrange("(p t) c -> t p c", t=PACK)
-
-        q_win = []
-        for t in range(PACK):
-            win = sbuf(f"q_win{t}", [P, T], F32)
-            nc.vector.memset(win[:], 0.0)
-            q_win.append(win)
-
-        wb_codes = sbuf("wb_codes", [P, 2 * N], U8, tag="wb_xa_codes")
-        wb_scale = sbuf("wb_scale", [P, N], U8, tag="wb_xa_scale")
-        nc.vector.tensor_copy(
-            out=wb_codes[:].bitcast(U16).rearrange("p (t m) -> p t m", t=PACK),
-            in_=wb_raw[:].bitcast(U16).rearrange("p (m t) -> p t m", t=PACK),
-        )
-        nc.vector.tensor_copy(
-            out=wb_scale[:].rearrange("p (t m) -> p t m", t=PACK),
-            in_=wb_scale_raw[:].rearrange("p (m t) -> p t m", t=PACK),
-        )
+            load_scale_rows(wb_scale_raw, wb_scales[0], q)
 
         wa_raw = []
         for z, tag in enumerate(("wb_wa_res", "scale_wa_q")):
@@ -93,31 +74,53 @@ def tile_moe_heads_of_two_experts_pl_kernel(
             )
             wa_raw.append(raw)
 
-        q_bank = []
-        for t in range(PACK):
-            bank = psum.tile([P, J], F32, name=f"q_bank{t}")
+        res_rows = res.rearrange("(p t) c -> p t c", t=PACK)
+        out_rows = out_0.rearrange("(p t) c -> t p c", t=PACK)
+
+        q_win = [sbuf("q_win0", [P, T], F32)]
+        nc.vector.memset(q_win[0][:], 0.0)
+
+        wb_codes = sbuf("wb_codes", [P, 2 * N], U8, tag="wb_xa_codes")
+        wb_scale = sbuf("wb_scale", [P, N], U8, tag="wb_xa_scale")
+        nc.vector.tensor_copy(
+            out=wb_codes[:].bitcast(U16).rearrange("p (t m) -> p t m", t=PACK),
+            in_=wb_raw[:].bitcast(U16).rearrange("p (m t) -> p t m", t=PACK),
+        )
+        for lo, hi in ((0, 1), (1, PACK)):
+            nc.vector.tensor_copy(
+                out=wb_scale[:].rearrange("p (t m) -> p t m", t=PACK)[:, lo:hi, :],
+                in_=wb_scale_raw[:].rearrange("p (m t) -> p t m", t=PACK)[:, lo:hi, :],
+            )
+
+        def q_product(t, lo, hi, bank_tag):
+            bank = psum.tile([P, hi - lo], F32, name=f"q_bank{t}_{lo}", tag=bank_tag)
             nc.tensor.matmul_mx(
                 out=bank[:],
                 lhsT=wb_codes[:, 2 * P * t : 2 * P * (t + 1)].bitcast(FP4X4),
                 lhsT_scale=wb_scale[:, P * t : P * (t + 1)],
-                rhs=xb_codes[:].bitcast(FP8X4),
-                rhs_scale=xb_scale[:],
+                rhs=xb_codes[:, lo:hi].bitcast(FP8X4),
+                rhs_scale=xb_scale[:, lo:hi],
                 start=True,
                 stop=True,
             )
-            q_bank.append(bank)
+            return bank
 
-        def scatter_q(t, tag):
-            slots = sbuf(f"q_slots{t}", [P, J], F32, tag=tag)
-            nc.scalar.copy(out=slots[:], in_=q_bank[t][:])
-            nc.vector.tensor_copy(out=q_win[t][:].indirect(list_q[:]), in_=slots[:])
+        def scatter_q(t, lo, hi, bank, tag=None):
+            slots = sbuf(f"q_slots{t}_{lo}", [P, hi - lo], F32, tag=tag)
+            nc.scalar.copy(out=slots[:], in_=bank[:])
+            nc.vector.tensor_copy(out=q_win[t][:].indirect(list_q[:, lo // 16 : hi // 16]), in_=slots[:])
 
-        for t in range(PACK - 1):
-            scatter_q(t, None)
+        pieces = [(0, 0, J // 2), (0, J // 2, J), (1, 0, J), (2, 0, J), (3, 0, J)]
+        q_bank = [q_product(*piece, f"bank{b}") for b, piece in enumerate(pieces)]
+        for t in range(1, PACK):
+            q_win.append(sbuf(f"q_win{t}", [P, T], F32, tag=f"then_q_win{t}"))
+            nc.gpsimd.memset(q_win[t][:], 0.0)
+        scatter_q(*pieces[0], q_bank[0], tag="then_p_win1")
+        for piece, bank in zip(pieces[1:-1], q_bank[1:]):
+            scatter_q(*piece, bank)
 
         xa_codes = sbuf("xa_codes", [P, PASSES, 2 * J], U8, tag="wb_xa_codes")
         xa_scale = sbuf("xa_scale", [P, PASSES, J], U8, tag="wb_xa_scale")
-        nc.gpsimd.memset(xa_scale[:].bitcast(I32), 0)
         nc.sync.dma_start(out=xa_codes[:].bitcast(I32), in_=xa_words.bitcast(I32).rearrange("z p w -> p z w"))
         for q in range(QUADS):
             nc.sync.dma_start(
@@ -127,7 +130,7 @@ def tile_moe_heads_of_two_experts_pl_kernel(
 
         p_win = []
         for b in range(2):
-            win = sbuf(f"p_win{b}", [P, T], F32, tag=f"xb_win{b}")
+            win = sbuf(f"p_win{b}", [P, T], F32, tag=f"then_p_win{b}")
             nc.gpsimd.memset(win[:], 0.0)
             p_win.append(win)
 
@@ -147,11 +150,11 @@ def tile_moe_heads_of_two_experts_pl_kernel(
         res_raw = sbuf("res_raw", [P, PACK, T], F32, tag="wb_wa_res")
         nc.sync.dma_start(out=res_raw[:], in_=res_rows)
 
-        scatter_q(PACK - 1, "scale_wa_q")
+        scatter_q(*pieces[-1], q_bank[-1], tag="scale_wa_q")
 
         p_slots = []
         for t in range(PACK):
-            bank = psum.tile([P, J], F32, name=f"p_bank{t}")
+            bank = psum.tile([P, J], F32, name=f"p_bank{t}", tag=f"bank{(5 + t) % 8}")
             for z in range(PASSES):
                 nc.tensor.matmul_mx(
                     out=bank[:],
@@ -173,8 +176,8 @@ def tile_moe_heads_of_two_experts_pl_kernel(
             res_scaled.append(scaled)
 
         y_pair = [sbuf(f"y_pair{u}", [P, 2, T], F32) for u in range(2)]
-        y_bf = [sbuf(f"y_bf{h}", [P, HALF, PACK], BF16) for h in range(2)]
-        halves = [slice(h * HALF, (h + 1) * HALF) for h in range(2)]
+        y_bf = [sbuf(f"y_bf{c}", [P, CHUNK, PACK], BF16) for c in range(CHUNKS)]
+        chunks = [slice(c * CHUNK, (c + 1) * CHUNK) for c in range(CHUNKS)]
         larger = [sbuf(f"larger{t}", [P, T], F32) for t in range(PACK)]
 
         def scatter_p(t, lo, hi):
@@ -194,37 +197,61 @@ def tile_moe_heads_of_two_experts_pl_kernel(
             combine(t - 1)
             scatter_p(t, LEAD, J)
             if t == 2:
-                for h in range(2):
+                for c in range(CHUNKS):
                     nc.scalar.copy(
-                        out=y_bf[h][:, :, 0:2], in_=y_pair[0][:, :, halves[h]].rearrange("p e c -> p c e")
+                        out=y_bf[c][:, :, 0:2], in_=y_pair[0][:, :, chunks[c]].rearrange("p e c -> p c e")
                     )
 
         last = PACK - 1
         y = y_pair[1][:, 1, :]
-        for cols in halves:
+        y_scale = sbuf("y_scale", [P, T], U8)
+        y_codes = sbuf("y_codes", [P, T], U32)
+        words_out = out_1[0].rearrange("p c t -> p (c t)").bitcast(I32)
+
+        def last_max(c):
+            cols = chunks[c]
             nc.vector.tensor_tensor(
                 out=larger[last][:, cols], in0=p_win[1][:, cols], in1=q_win[last][:, cols], op=ALU.max
             )
-        for cols in halves:
+
+        def last_add(c):
+            cols = chunks[c]
             nc.vector.tensor_tensor(
                 out=y[:, cols], in0=larger[last][:, cols], in1=res_scaled[last][:, cols], op=ALU.add
             )
-            nc.sync.dma_start(out=out_rows[last][:, cols], in_=y[:, cols])
 
-        nc.scalar.copy(out=y_bf[0][:, :, 2:4], in_=y_pair[1][:, :, halves[0]].rearrange("p e c -> p c e"))
-        nc.vector.tensor_copy(out=y_bf[1][:, :, 2:4], in_=y_pair[1][:, :, halves[1]].rearrange("p e c -> p c e"))
+        def round_pair(c, copy):
+            copy(out=y_bf[c][:, :, 2:4], in_=y_pair[1][:, :, chunks[c]].rearrange("p e c -> p c e"))
 
-        y_scale = sbuf("y_scale", [P, T], U8)
-        words_out = out_1[0].rearrange("p c t -> p (c t)").bitcast(I32)
-        for h in (1, 0):
-            codes = sbuf(f"y_codes{h}", [P, HALF], U32)
+        def quantize(c):
             nc.vector.quantize_mx(
-                out=codes[:].bitcast(FP8X4),
-                scales=y_scale[:, halves[h]],
-                in_=y_bf[h][:].rearrange("p c t -> p (c t)"),
+                out=y_codes[:, chunks[c]].bitcast(FP8X4),
+                scales=y_scale[:, chunks[c]],
+                in_=y_bf[c][:].rearrange("p c t -> p (c t)"),
             )
-            nc.sync.dma_start(out=words_out[:, halves[h]], in_=codes[:].bitcast(I32))
+
+        def store_words(lo, hi):
+            nc.sync.dma_start(
+                out=words_out[:, lo * CHUNK : hi * CHUNK], in_=y_codes[:, lo * CHUNK : hi * CHUNK].bitcast(I32)
+            )
+
+        last_max(0)
+        for c in range(CHUNKS):
+            if c + 1 < CHUNKS:
+                last_max(c + 1)
+            last_add(c)
+            if c + 1 < CHUNKS:
+                round_pair(c, nc.scalar.copy)
+        nc.sync.dma_start(out=out_rows[last], in_=y)
+        quantize(0)
+        round_pair(3, nc.vector.tensor_copy)
+        quantize(1)
+        store_words(0, 2)
+        quantize(3)
+        store_words(3, 4)
+        quantize(2)
+        store_words(2, 3)
         for q in range(QUADS):
-            nc.scalar.dma_start(
+            (nc.scalar if q < 3 else nc.sync).dma_start(
                 out=out_2[0, 4 * q : 4 * q + 4, :].bitcast(I32), in_=y_scale[32 * q : 32 * q + 4, :].bitcast(I32)
             )

@@ -21,6 +21,9 @@ PACK = 4
 K_PASS = P * PACK
 PASSES = K // K_PASS
 QUADS = 4
+BANKS = 8
+PER_COLUMN = 16
+RES_FACTOR = 0.3
 CHUNKS = 4
 CHUNK = T // CHUNKS
 LEAD = 128
@@ -38,36 +41,41 @@ def tile_moe_heads_of_two_experts_pl_kernel(
         def sbuf(name, shape, dtype, tag=None):
             return sb.tile(shape, dtype, name=name, tag=tag or name, align_bytes=64)
 
-        list_p = lists.tile([P, J // 16], U16, name="list_p")
-        list_q = lists.tile([P, J // 16], U16, name="list_q")
+        def scale_partitions(g):
+            return slice(32 * g, 32 * g + 4)
 
-        wb_raw = sbuf("wb_raw", [P, 2 * N], U8, tag="then_q_win1")
-        wb_scale_raw = sbuf("wb_scale_raw", [P, N], U8, tag="then_q_win2")
-        xb_codes = sbuf("xb_codes", [P, J], U32, tag="then_q_win3")
-        xb_scale = sbuf("xb_scale", [P, J], U8, tag="then_p_win0")
+        def scale_rows(g):
+            return slice(4 * g, 4 * g + 4)
 
-        nc.gpsimd.memset(wb_scale_raw[:].bitcast(I32), 0)
+        def list_columns(lo, hi):
+            return slice(lo // PER_COLUMN, hi // PER_COLUMN)
 
-        def load_scale_rows(plane, rows, q):
-            nc.sync.dma_start(
-                out=plane[32 * q : 32 * q + 4, :].bitcast(I32), in_=rows[4 * q : 4 * q + 4, :].bitcast(I32)
-            )
+        list_p = lists.tile([P, J // PER_COLUMN], U16, name="list_p")
+        list_q = lists.tile([P, J // PER_COLUMN], U16, name="list_q")
+
+        wb_raw = sbuf("wb_raw", [P, 2 * N], U8)
+        wb_scale_raw = sbuf("wb_scale_raw", [P, N], U8)
+        xb_codes = sbuf("xb_codes", [P, J], U32, tag="xb_codes_then_p_win1")
+        xb_scale = sbuf("xb_scale", [P, J], U8, tag="xb_scale_then_p_win0")
+
+        nc.vector.memset(wb_scale_raw[:].bitcast(I32), 0)
+
+        def load_scale_rows(plane, rows, g):
+            nc.sync.dma_start(out=plane[scale_partitions(g), :].bitcast(I32), in_=rows[scale_rows(g), :].bitcast(I32))
 
         nc.sync.dma_start(list_q[:], offs2)
         nc.sync.dma_start(list_p[:], offs)
-        for q in range(2):
-            load_scale_rows(xb_scale, xb_scales[0], q)
+        for g in range(QUADS // 2):
+            load_scale_rows(xb_scale, xb_scales[0], g)
         nc.sync.dma_start(out=wb_raw[:].bitcast(I32), in_=wb_words[0].bitcast(I32))
-        nc.sync.dma_start(
-            out=xb_codes[:].bitcast(I32), in_=xb_words[0].rearrange("p n t -> p (n t)").bitcast(I32)
-        )
-        for q in range(2, QUADS):
-            load_scale_rows(xb_scale, xb_scales[0], q)
-        for q in range(QUADS):
-            load_scale_rows(wb_scale_raw, wb_scales[0], q)
+        nc.sync.dma_start(out=xb_codes[:].bitcast(I32), in_=xb_words[0].rearrange("p n t -> p (n t)").bitcast(I32))
+        for g in range(QUADS // 2, QUADS):
+            load_scale_rows(xb_scale, xb_scales[0], g)
+        for g in range(QUADS):
+            load_scale_rows(wb_scale_raw, wb_scales[0], g)
 
         wa_raw = []
-        for z, tag in enumerate(("wb_wa_res", "scale_wa_q")):
+        for z, tag in enumerate(("wa_raw0_then_res", "wa_raw1_then_last_q_slots")):
             raw = sbuf(f"wa_raw{z}", [P, PACK, N], F32, tag=tag)
             nc.sync.dma_start(
                 out=raw[:], in_=wa[z * K_PASS : (z + 1) * K_PASS, :].rearrange("(p j) n -> p j n", j=PACK)
@@ -77,11 +85,13 @@ def tile_moe_heads_of_two_experts_pl_kernel(
         res_rows = res.rearrange("(p t) c -> p t c", t=PACK)
         out_rows = out_0.rearrange("(p t) c -> t p c", t=PACK)
 
-        q_win = [sbuf("q_win0", [P, T], F32)]
-        nc.vector.memset(q_win[0][:], 0.0)
+        q_win = [sbuf(f"q_win{t}", [P, T], F32) for t in range(PACK)]
+        nc.gpsimd.memset(q_win[0][:], 0.0)
+        for win in q_win[1:]:
+            nc.vector.memset(win[:], 0.0)
 
-        wb_codes = sbuf("wb_codes", [P, 2 * N], U8, tag="wb_xa_codes")
-        wb_scale = sbuf("wb_scale", [P, N], U8, tag="wb_xa_scale")
+        wb_codes = sbuf("wb_codes", [P, 2 * N], U8, tag="wb_codes_then_xa_codes")
+        wb_scale = sbuf("wb_scale", [P, N], U8, tag="wb_scale_then_xa_scale")
         nc.vector.tensor_copy(
             out=wb_codes[:].bitcast(U16).rearrange("p (t m) -> p t m", t=PACK),
             in_=wb_raw[:].bitcast(U16).rearrange("p (m t) -> p t m", t=PACK),
@@ -108,29 +118,25 @@ def tile_moe_heads_of_two_experts_pl_kernel(
         def scatter_q(t, lo, hi, bank, tag=None):
             slots = sbuf(f"q_slots{t}_{lo}", [P, hi - lo], F32, tag=tag)
             nc.scalar.copy(out=slots[:], in_=bank[:])
-            nc.vector.tensor_copy(out=q_win[t][:].indirect(list_q[:, lo // 16 : hi // 16]), in_=slots[:])
+            nc.vector.tensor_copy(out=q_win[t][:].indirect(list_q[:, list_columns(lo, hi)]), in_=slots[:])
 
-        pieces = [(0, 0, J // 2), (0, J // 2, J), (1, 0, J), (2, 0, J), (3, 0, J)]
-        q_bank = [q_product(*piece, f"bank{b}") for b, piece in enumerate(pieces)]
-        for t in range(1, PACK):
-            q_win.append(sbuf(f"q_win{t}", [P, T], F32, tag=f"then_q_win{t}"))
-            nc.gpsimd.memset(q_win[t][:], 0.0)
-        scatter_q(*pieces[0], q_bank[0], tag="then_p_win1")
-        for piece, bank in zip(pieces[1:-1], q_bank[1:]):
+        q_pieces = [(0, 0, J // 2), (1, 0, J), (0, J // 2, J), (2, 0, J), (3, 0, J)]
+        q_bank = [q_product(*piece, f"bank{b}") for b, piece in enumerate(q_pieces)]
+        for piece, bank in zip(q_pieces[:-1], q_bank):
             scatter_q(*piece, bank)
 
-        xa_codes = sbuf("xa_codes", [P, PASSES, 2 * J], U8, tag="wb_xa_codes")
-        xa_scale = sbuf("xa_scale", [P, PASSES, J], U8, tag="wb_xa_scale")
+        xa_codes = sbuf("xa_codes", [P, PASSES, 2 * J], U8, tag="wb_codes_then_xa_codes")
+        xa_scale = sbuf("xa_scale", [P, PASSES, J], U8, tag="wb_scale_then_xa_scale")
         nc.sync.dma_start(out=xa_codes[:].bitcast(I32), in_=xa_words.bitcast(I32).rearrange("z p w -> p z w"))
-        for q in range(QUADS):
+        for g in range(QUADS):
             nc.sync.dma_start(
-                out=xa_scale[32 * q : 32 * q + 4, :, :].bitcast(I32),
-                in_=xa_scales[:, 4 * q : 4 * q + 4, :].bitcast(I32).rearrange("z r w -> r z w"),
+                out=xa_scale[scale_partitions(g), :, :].bitcast(I32),
+                in_=xa_scales[:, scale_rows(g), :].bitcast(I32).rearrange("z r w -> r z w"),
             )
 
         p_win = []
-        for b in range(2):
-            win = sbuf(f"p_win{b}", [P, T], F32, tag=f"then_p_win{b}")
+        for b, tag in enumerate(("xb_scale_then_p_win0", "xb_codes_then_p_win1")):
+            win = sbuf(f"p_win{b}", [P, T], F32, tag=tag)
             nc.gpsimd.memset(win[:], 0.0)
             p_win.append(win)
 
@@ -147,14 +153,14 @@ def tile_moe_heads_of_two_experts_pl_kernel(
             wa_codes.append(codes)
             wa_scale.append(scale)
 
-        res_raw = sbuf("res_raw", [P, PACK, T], F32, tag="wb_wa_res")
+        res_raw = sbuf("res_raw", [P, PACK, T], F32, tag="wa_raw0_then_res")
         nc.sync.dma_start(out=res_raw[:], in_=res_rows)
 
-        scatter_q(*pieces[-1], q_bank[-1], tag="scale_wa_q")
+        scatter_q(*q_pieces[-1], q_bank[-1], tag="wa_raw1_then_last_q_slots")
 
         p_slots = []
         for t in range(PACK):
-            bank = psum.tile([P, J], F32, name=f"p_bank{t}", tag=f"bank{(5 + t) % 8}")
+            bank = psum.tile([P, J], F32, name=f"p_bank{t}", tag=f"bank{(len(q_pieces) + t) % BANKS}")
             for z in range(PASSES):
                 nc.tensor.matmul_mx(
                     out=bank[:],
@@ -172,17 +178,17 @@ def tile_moe_heads_of_two_experts_pl_kernel(
         res_scaled = []
         for t in range(PACK):
             scaled = sbuf(f"res_scaled{t}", [P, T], F32)
-            nc.scalar.activation(out=scaled[:], in_=res_raw[:, t, :], func=COPY, scale=0.3)
+            nc.scalar.activation(out=scaled[:], in_=res_raw[:, t, :], func=COPY, scale=RES_FACTOR)
             res_scaled.append(scaled)
 
-        y_pair = [sbuf(f"y_pair{u}", [P, 2, T], F32) for u in range(2)]
+        y_pair = [sbuf(f"y_pair{u}", [P, 2, T], F32) for u in range(PACK // 2)]
         y_bf = [sbuf(f"y_bf{c}", [P, CHUNK, PACK], BF16) for c in range(CHUNKS)]
         chunks = [slice(c * CHUNK, (c + 1) * CHUNK) for c in range(CHUNKS)]
         larger = [sbuf(f"larger{t}", [P, T], F32) for t in range(PACK)]
 
         def scatter_p(t, lo, hi):
             nc.vector.tensor_copy(
-                out=p_win[t % 2][:].indirect(list_p[:, lo // 16 : hi // 16]), in_=p_slots[t][:, lo:hi]
+                out=p_win[t % 2][:].indirect(list_p[:, list_columns(lo, hi)]), in_=p_slots[t][:, lo:hi]
             )
 
         def combine(t):
@@ -191,19 +197,20 @@ def tile_moe_heads_of_two_experts_pl_kernel(
             nc.gpsimd.tensor_tensor(out=y, in0=larger[t][:], in1=res_scaled[t][:], op=ALU.add)
             nc.sync.dma_start(out=out_rows[t], in_=y)
 
+        def round_pair(u, c, copy):
+            copy(out=y_bf[c][:, :, 2 * u : 2 * u + 2], in_=y_pair[u][:, :, chunks[c]].rearrange("p e c -> p c e"))
+
         scatter_p(0, 0, J)
         for t in range(1, PACK):
             scatter_p(t, 0, LEAD)
             combine(t - 1)
             scatter_p(t, LEAD, J)
-            if t == 2:
+            if t - 1 == 1:
                 for c in range(CHUNKS):
-                    nc.scalar.copy(
-                        out=y_bf[c][:, :, 0:2], in_=y_pair[0][:, :, chunks[c]].rearrange("p e c -> p c e")
-                    )
+                    round_pair(0, c, nc.scalar.copy)
 
         last = PACK - 1
-        y = y_pair[1][:, 1, :]
+        y_last = y_pair[last // 2][:, last % 2, :]
         y_scale = sbuf("y_scale", [P, T], U8)
         y_codes = sbuf("y_codes", [P, T], U32)
         words_out = out_1[0].rearrange("p c t -> p (c t)").bitcast(I32)
@@ -211,17 +218,14 @@ def tile_moe_heads_of_two_experts_pl_kernel(
         def last_max(c):
             cols = chunks[c]
             nc.vector.tensor_tensor(
-                out=larger[last][:, cols], in0=p_win[1][:, cols], in1=q_win[last][:, cols], op=ALU.max
+                out=larger[last][:, cols], in0=p_win[last % 2][:, cols], in1=q_win[last][:, cols], op=ALU.max
             )
 
         def last_add(c):
             cols = chunks[c]
             nc.vector.tensor_tensor(
-                out=y[:, cols], in0=larger[last][:, cols], in1=res_scaled[last][:, cols], op=ALU.add
+                out=y_last[:, cols], in0=larger[last][:, cols], in1=res_scaled[last][:, cols], op=ALU.add
             )
-
-        def round_pair(c, copy):
-            copy(out=y_bf[c][:, :, 2:4], in_=y_pair[1][:, :, chunks[c]].rearrange("p e c -> p c e"))
 
         def quantize(c):
             nc.vector.quantize_mx(
@@ -230,10 +234,9 @@ def tile_moe_heads_of_two_experts_pl_kernel(
                 in_=y_bf[c][:].rearrange("p c t -> p (c t)"),
             )
 
-        def store_words(lo, hi):
-            nc.sync.dma_start(
-                out=words_out[:, lo * CHUNK : hi * CHUNK], in_=y_codes[:, lo * CHUNK : hi * CHUNK].bitcast(I32)
-            )
+        def store_words(c_lo, c_hi):
+            cols = slice(c_lo * CHUNK, c_hi * CHUNK)
+            nc.sync.dma_start(out=words_out[:, cols], in_=y_codes[:, cols].bitcast(I32))
 
         last_max(0)
         for c in range(CHUNKS):
@@ -241,17 +244,20 @@ def tile_moe_heads_of_two_experts_pl_kernel(
                 last_max(c + 1)
             last_add(c)
             if c + 1 < CHUNKS:
-                round_pair(c, nc.scalar.copy)
-        nc.sync.dma_start(out=out_rows[last], in_=y)
+                round_pair(1, c, nc.scalar.copy)
+            if c % 2 == 1:
+                half = slice((c - 1) * CHUNK, (c + 1) * CHUNK)
+                nc.sync.dma_start(out=out_rows[last][:, half], in_=y_last[:, half])
+
         quantize(0)
-        round_pair(3, nc.vector.tensor_copy)
+        round_pair(1, 3, nc.vector.tensor_copy)
         quantize(1)
         store_words(0, 2)
         quantize(3)
         store_words(3, 4)
         quantize(2)
         store_words(2, 3)
-        for q in range(QUADS):
-            (nc.scalar if q < 3 else nc.sync).dma_start(
-                out=out_2[0, 4 * q : 4 * q + 4, :].bitcast(I32), in_=y_scale[32 * q : 32 * q + 4, :].bitcast(I32)
+        for g in range(QUADS):
+            (nc.scalar if g < QUADS - 1 else nc.sync).dma_start(
+                out=out_2[0, scale_rows(g), :].bitcast(I32), in_=y_scale[scale_partitions(g), :].bitcast(I32)
             )

from contextlib import ExitStack

import concourse.mybir as mybir

K, L, T, J, N = 1024, 512, 1024, 512, 512
FLOPS = 2 * (K + L) * N * J

F32 = mybir.dt.float32
BF16 = mybir.dt.bfloat16
I32 = mybir.dt.int32
U32 = mybir.dt.uint32
U16 = mybir.dt.uint16
U8 = mybir.dt.uint8
FP8X4 = mybir.dt.float8_e4m3fn_x4
FP4X4 = mybir.dt.float4_e2m1fn_x4
ALU = mybir.AluOpType
COPY = mybir.ActivationFunctionType.Copy

P = 128
PACK = 4
K_PASS = P * PACK
PASSES = K // K_PASS
QUADS = 4
BANKS = 8
PER_COLUMN = 16
RES_FACTOR = 0.3
CHUNKS = 4
CHUNK = T // CHUNKS
LEAD = 128


def tile_moe_heads_of_two_experts_pl_kernel(
    tc, xa_words, xa_scales, wa, xb_words, xb_scales, wb_words, wb_scales, res, offs, offs2, out_0, out_1, out_2
):
    nc = tc.nc
    with ExitStack() as ctx:
        lists = ctx.enter_context(tc.tile_pool(name="lists", bufs=1))
        sb = ctx.enter_context(tc.tile_pool(name="sb", bufs=1))
        psum = ctx.enter_context(tc.psum_pool(name="psum", bufs=1))

        def sbuf(name, shape, dtype, tag=None):
            return sb.tile(shape, dtype, name=name, tag=tag or name, align_bytes=64)

        def scale_partitions(g):
            return slice(32 * g, 32 * g + 4)

        def scale_rows(g):
            return slice(4 * g, 4 * g + 4)

        def list_columns(lo, hi):
            return slice(lo // PER_COLUMN, hi // PER_COLUMN)

        list_p = lists.tile([P, J // PER_COLUMN], U16, name="list_p")
        list_q = lists.tile([P, J // PER_COLUMN], U16, name="list_q")

        wb_raw = sbuf("wb_raw", [P, 2 * N], U8)
        wb_scale_raw = sbuf("wb_scale_raw", [P, N], U8)
        xb_codes = sbuf("xb_codes", [P, J], U32, tag="xb_codes_then_p_win1")
        xb_scale = sbuf("xb_scale", [P, J], U8, tag="xb_scale_then_p_win0")

        nc.vector.memset(wb_scale_raw[:].bitcast(I32), 0)

        def load_scale_rows(plane, rows, g):
            nc.sync.dma_start(out=plane[scale_partitions(g), :].bitcast(I32), in_=rows[scale_rows(g), :].bitcast(I32))

        nc.sync.dma_start(list_q[:], offs2)
        nc.sync.dma_start(list_p[:], offs)
        for g in range(QUADS // 2):
            load_scale_rows(xb_scale, xb_scales[0], g)
        nc.sync.dma_start(out=wb_raw[:].bitcast(I32), in_=wb_words[0].bitcast(I32))
        nc.sync.dma_start(out=xb_codes[:].bitcast(I32), in_=xb_words[0].rearrange("p n t -> p (n t)").bitcast(I32))
        for g in range(QUADS // 2, QUADS):
            load_scale_rows(xb_scale, xb_scales[0], g)
        for g in range(QUADS):
            load_scale_rows(wb_scale_raw, wb_scales[0], g)

        wa_raw = []
        for z, tag in enumerate(("wa_raw0_then_res", "wa_raw1_then_last_q_slots")):
            raw = sbuf(f"wa_raw{z}", [P, PACK, N], F32, tag=tag)
            nc.sync.dma_start(
                out=raw[:], in_=wa[z * K_PASS : (z + 1) * K_PASS, :].rearrange("(p j) n -> p j n", j=PACK)
            )
            wa_raw.append(raw)

        res_rows = res.rearrange("(p t) c -> p t c", t=PACK)
        out_rows = out_0.rearrange("(p t) c -> t p c", t=PACK)

        q_win = [sbuf(f"q_win{t}", [P, T], F32) for t in range(PACK)]
        nc.gpsimd.memset(q_win[0][:], 0.0)
        for win in q_win[1:]:
            nc.vector.memset(win[:], 0.0)

        wb_codes = sbuf("wb_codes", [P, 2 * N], U8, tag="wb_codes_then_xa_codes")
        wb_scale = sbuf("wb_scale", [P, N], U8, tag="wb_scale_then_xa_scale")
        nc.vector.tensor_copy(
            out=wb_codes[:].bitcast(U16).rearrange("p (t m) -> p t m", t=PACK),
            in_=wb_raw[:].bitcast(U16).rearrange("p (m t) -> p t m", t=PACK),
        )
        for lo, hi in ((0, 1), (1, PACK)):
            nc.vector.tensor_copy(
                out=wb_scale[:].rearrange("p (t m) -> p t m", t=PACK)[:, lo:hi, :],
                in_=wb_scale_raw[:].rearrange("p (m t) -> p t m", t=PACK)[:, lo:hi, :],
            )

        def q_product(t, lo, hi, bank_tag):
            bank = psum.tile([P, hi - lo], F32, name=f"q_bank{t}_{lo}", tag=bank_tag)
            nc.tensor.matmul_mx(
                out=bank[:],
                lhsT=wb_codes[:, 2 * P * t : 2 * P * (t + 1)].bitcast(FP4X4),
                lhsT_scale=wb_scale[:, P * t : P * (t + 1)],
                rhs=xb_codes[:, lo:hi].bitcast(FP8X4),
                rhs_scale=xb_scale[:, lo:hi],
                start=True,
                stop=True,
            )
            return bank

        def scatter_q(t, lo, hi, bank, tag=None):
            slots = sbuf(f"q_slots{t}_{lo}", [P, hi - lo], F32, tag=tag)
            nc.scalar.copy(out=slots[:], in_=bank[:])
            nc.vector.tensor_copy(out=q_win[t][:].indirect(list_q[:, list_columns(lo, hi)]), in_=slots[:])

        q_pieces = [(0, 0, J // 2), (1, 0, J), (0, J // 2, J), (2, 0, J), (3, 0, J)]
        q_bank = [q_product(*piece, f"bank{b}") for b, piece in enumerate(q_pieces)]
        for piece, bank in zip(q_pieces[:-1], q_bank):
            scatter_q(*piece, bank)

        xa_codes = sbuf("xa_codes", [P, PASSES, 2 * J], U8, tag="wb_codes_then_xa_codes")
        xa_scale = sbuf("xa_scale", [P, PASSES, J], U8, tag="wb_scale_then_xa_scale")
        nc.sync.dma_start(out=xa_codes[:].bitcast(I32), in_=xa_words.bitcast(I32).rearrange("z p w -> p z w"))
        for g in range(QUADS):
            nc.sync.dma_start(
                out=xa_scale[scale_partitions(g), :, :].bitcast(I32),
                in_=xa_scales[:, scale_rows(g), :].bitcast(I32).rearrange("z r w -> r z w"),
            )

        p_win = []
        for b, tag in enumerate(("xb_scale_then_p_win0", "xb_codes_then_p_win1")):
            win = sbuf(f"p_win{b}", [P, T], F32, tag=tag)
            nc.gpsimd.memset(win[:], 0.0)
            p_win.append(win)

        wa_codes, wa_scale = [], []
        for z in range(PASSES):
            grouped = sbuf(f"wa_grouped{z}", [P, PACK * N], BF16)
            nc.scalar.copy(
                out=grouped[:].rearrange("p (t m j) -> p m t j", t=PACK, j=PACK),
                in_=wa_raw[z][:].rearrange("p j (m t) -> p m t j", t=PACK),
            )
            codes = sbuf(f"wa_codes{z}", [P, N], U32)
            scale = sbuf(f"wa_scale{z}", [P, N], U8)
            nc.vector.quantize_mx(out=codes[:].bitcast(FP8X4), scales=scale[:], in_=grouped[:])
            wa_codes.append(codes)
            wa_scale.append(scale)

        res_raw = sbuf("res_raw", [P, PACK, T], F32, tag="wa_raw0_then_res")
        nc.sync.dma_start(out=res_raw[:], in_=res_rows)

        scatter_q(*q_pieces[-1], q_bank[-1], tag="wa_raw1_then_last_q_slots")

        p_slots = []
        for t in range(PACK):
            bank = psum.tile([P, J], F32, name=f"p_bank{t}", tag=f"bank{(len(q_pieces) + t) % BANKS}")
            for z in range(PASSES):
                nc.tensor.matmul_mx(
                    out=bank[:],
                    lhsT=wa_codes[z][:, P * t : P * (t + 1)].bitcast(FP8X4),
                    lhsT_scale=wa_scale[z][:, P * t : P * (t + 1)],
                    rhs=xa_codes[:, z, :].bitcast(FP4X4),
                    rhs_scale=xa_scale[:, z, :],
                    start=(z == 0),
                    stop=(z == PASSES - 1),
                )
            slots = sbuf(f"p_slots{t}", [P, J], F32)
            nc.scalar.copy(out=slots[:], in_=bank[:])
            p_slots.append(slots)

        res_scaled = []
        for t in range(PACK):
            scaled = sbuf(f"res_scaled{t}", [P, T], F32)
            nc.scalar.activation(out=scaled[:], in_=res_raw[:, t, :], func=COPY, scale=RES_FACTOR)
            res_scaled.append(scaled)

        y_pair = [sbuf(f"y_pair{u}", [P, 2, T], F32) for u in range(PACK // 2)]
        y_bf = [sbuf(f"y_bf{c}", [P, CHUNK, PACK], BF16) for c in range(CHUNKS)]
        chunks = [slice(c * CHUNK, (c + 1) * CHUNK) for c in range(CHUNKS)]
        larger = [sbuf(f"larger{t}", [P, T], F32) for t in range(PACK)]

        def scatter_p(t, lo, hi):
            nc.vector.tensor_copy(
                out=p_win[t % 2][:].indirect(list_p[:, list_columns(lo, hi)]), in_=p_slots[t][:, lo:hi]
            )

        def combine(t):
            y = y_pair[t // 2][:, t % 2, :]
            nc.vector.tensor_tensor(out=larger[t][:], in0=p_win[t % 2][:], in1=q_win[t][:], op=ALU.max)
            nc.gpsimd.tensor_tensor(out=y, in0=larger[t][:], in1=res_scaled[t][:], op=ALU.add)
            nc.sync.dma_start(out=out_rows[t], in_=y)

        def round_pair(u, c, copy):
            copy(out=y_bf[c][:, :, 2 * u : 2 * u + 2], in_=y_pair[u][:, :, chunks[c]].rearrange("p e c -> p c e"))

        scatter_p(0, 0, J)
        for t in range(1, PACK):
            scatter_p(t, 0, LEAD)
            combine(t - 1)
            scatter_p(t, LEAD, J)
            if t - 1 == 1:
                for c in range(CHUNKS):
                    round_pair(0, c, nc.scalar.copy)

        last = PACK - 1
        y_last = y_pair[last // 2][:, last % 2, :]
        y_scale = sbuf("y_scale", [P, T], U8)
        y_codes = sbuf("y_codes", [P, T], U32)
        words_out = out_1[0].rearrange("p c t -> p (c t)").bitcast(I32)

        def last_max(c):
            cols = chunks[c]
            nc.vector.tensor_tensor(
                out=larger[last][:, cols], in0=p_win[last % 2][:, cols], in1=q_win[last][:, cols], op=ALU.max
            )

        def last_add(c):
            cols = chunks[c]
            nc.vector.tensor_tensor(
                out=y_last[:, cols], in0=larger[last][:, cols], in1=res_scaled[last][:, cols], op=ALU.add
            )

        def quantize(c):
            nc.vector.quantize_mx(
                out=y_codes[:, chunks[c]].bitcast(FP8X4),
                scales=y_scale[:, chunks[c]],
                in_=y_bf[c][:].rearrange("p c t -> p (c t)"),
            )

        def store_words(c_lo, c_hi):
            cols = slice(c_lo * CHUNK, c_hi * CHUNK)
            nc.sync.dma_start(out=words_out[:, cols], in_=y_codes[:, cols].bitcast(I32))

        last_max(0)
        for c in range(CHUNKS):
            if c + 1 < CHUNKS:
                last_max(c + 1)
            last_add(c)
            if c + 1 < CHUNKS:
                round_pair(1, c, nc.scalar.copy)
            if c % 2 == 1:
                half = slice((c - 1) * CHUNK, (c + 1) * CHUNK)
                nc.sync.dma_start(out=out_rows[last][:, half], in_=y_last[:, half])

        quantize(0)
        round_pair(1, 3, nc.vector.tensor_copy)
        quantize(1)
        store_words(0, 2)
        quantize(3)
        store_words(3, 4)
        quantize(2)
        store_words(2, 3)
        for g in range(QUADS):
            (nc.scalar if g < QUADS - 1 else nc.sync).dma_start(
                out=out_2[0, scale_rows(g), :].bitcast(I32), in_=y_scale[scale_partitions(g), :].bitcast(I32)
            )
